import numpy as np
import ml_dtypes


def mxq(x, axis, fmt="e4m3"):
    dtype, down = {"e4m3": (ml_dtypes.float8_e4m3fn, 7), "e5m2": (ml_dtypes.float8_e5m2, 14)}[fmt]
    v = np.moveaxis(np.asarray(x, np.float32).astype(ml_dtypes.bfloat16).astype(np.float64), axis, -1)
    blocks = v.reshape(v.shape[:-1] + (-1, 32))
    amax = np.abs(blocks).max(-1, keepdims=True)
    byte = np.maximum(np.where(amax > 0, np.frexp(amax)[1] - 1 + 127, 0) - down, 1)
    scale = np.exp2(byte - 127.0)
    codes = (blocks / scale).astype(np.float32).astype(dtype).astype(np.float64)
    return np.moveaxis((codes * scale).reshape(v.shape), -1, axis)


WIDE = False


def mx_kscale(k):
    if not WIDE:
        return np.ones(k)
    levels = np.array([10, -10, 5, -5, 0])
    if k % 512:
        return np.exp2(np.random.permutation(np.resize(levels, k // 32))).repeat(32)
    a = np.empty((k // 512, 16))
    for p in range(k // 512):
        a[p, :8] = np.random.permutation(np.resize(levels, 8))
        for g in range(8):
            far = levels[np.abs(levels - a[p, g]) >= 10]
            a[p, g + 8] = far[np.random.randint(len(far))]
    return np.exp2(a.ravel()).repeat(32)


def f64(x):
    return np.asarray(x).astype(np.float64)


def striped(idx):
    return np.tile(idx.reshape(-1, 16).T, (8, 1)).astype(np.uint16)


def unstriped(offs):
    return offs[:16].T.reshape(-1).astype(np.int64)


def striped8(idx):
    return np.concatenate([x.reshape(-1, 16).T for x in idx]).astype(np.uint16)


def runs(offs, k):
    lists = np.stack([offs[16 * r : 16 * r + 16].T.reshape(-1) for r in range(8)]).astype(np.int64)
    return lists[np.arange(k) % 512 // 64]


def pack_weight(w):
    k, n = w.shape
    w = f64(np.asarray(w, np.float32).astype(ml_dtypes.bfloat16)).reshape(k // 32, 32, n)
    amax = np.abs(w).max(1)
    byte = np.clip(np.where(amax > 0, np.frexp(amax)[1] - 1 + 127 - 7, 1), 1, 254)
    scaled = (w * np.exp2(127.0 - byte)[:, None, :]).reshape(k, n).astype(np.float32)
    words = np.ascontiguousarray(scaled.reshape(k // 512, 128, 4, n).transpose(0, 1, 3, 2)).astype(ml_dtypes.float8_e4m3fn).view(np.uint8)
    return words, np.ascontiguousarray(byte.astype(np.uint8).reshape(k // 512, 16, n))


def unpack_weight(words, scales):
    g, p, n, _ = words.shape
    vals = np.ascontiguousarray(words).view(ml_dtypes.float8_e4m3fn).astype(np.float64) * np.repeat(np.exp2(scales.astype(np.float64) - 127.0), 8, axis=1)[..., None]
    return vals.transpose(0, 1, 3, 2).reshape(g * 512, n)


def relu(v):
    return np.maximum(v, 0.0)

def planes(y):
    n, m = y.shape
    v = y.astype(np.float32).astype(ml_dtypes.bfloat16).astype(np.float64).reshape(n // 32, 32, m)
    top = np.abs(v).max(1)
    byte = np.clip(np.where(top > 0, np.frexp(top)[1] - 1 + 127 - 7, 1), 1, 254)
    codes = (v * np.exp2(127.0 - byte)[:, None, :]).reshape(n, m).astype(np.float32).astype(ml_dtypes.float8_e4m3fn).view(np.uint8)
    words = codes.reshape(n // 512, 128, 4, m).transpose(0, 1, 3, 2)
    return np.ascontiguousarray(words), np.ascontiguousarray(byte.astype(np.uint8).reshape(n // 512, 16, m))


K, T, S, N, H = 512, 2048, 512, 512, 512


def setup_inputs():
    n = np.random.standard_normal
    s = mx_kscale(K)[:, None]
    u = mx_kscale(H)
    packed_xT = pack_weight(n((K, T)) * s)
    packed_w3 = pack_weight(n((H, N)) / np.sqrt(H) / u[:, None])
    return {
        "x_words": packed_xT[0],
        "x_scales": packed_xT[1],
        "w1": (n((K, H)) / np.sqrt(K) / s * u).astype(np.float32),
        "w2": (n((H, H)) / np.sqrt(H) / u[:, None] * u).astype(np.float32),
        "w3_words": packed_w3[0],
        "w3_scales": packed_w3[1],
        "res": n((N, S)).astype(np.float32),
        "offs": striped(np.random.permutation(T)[:S]),
        "n1": striped8(np.stack([np.random.permutation(S) for _ in range(8)])),
        "n2": striped8(np.stack([np.random.permutation(S) for _ in range(8)])),
    }


def reference(x_words, x_scales, w1, w2, w3_words, w3_scales, res, offs, n1, n2):
    xq = unpack_weight(x_words, x_scales)[:, unstriped(offs)]
    y = mxq(f64(w1), 0, "e4m3").T @ xq
    z = relu(y - (y[np.arange(H)[:, None], runs(n1, H)]))
    h = mxq(f64(w2), 0, "e4m3").T @ mxq(z, 0, "e4m3")
    z2 = relu(h[np.arange(H)[:, None], runs(n2, H)] - h) - (0.25 * h)
    out_0 = f64(res) + (unpack_weight(w3_words, w3_scales).T @ mxq(z2, 0, "e4m3"))
    return (out_0,) + planes(out_0)

@@ -1,0 +1,240 @@
+from contextlib import ExitStack
+
+import concourse.mybir as mybir
+
+K, T, S, N, H = 512, 2048, 512, 512, 512
+FLOPS = 3 * 2 * 512 * 512 * 512
+
+F32 = mybir.dt.float32
+BF16 = mybir.dt.bfloat16
+I32 = mybir.dt.int32
+U32 = mybir.dt.uint32
+U16 = mybir.dt.uint16
+U8 = mybir.dt.uint8
+FP8X4 = mybir.dt.float8_e4m3fn_x4
+ALU = mybir.AluOpType
+COPY = mybir.ActivationFunctionType.Copy
+
+P = 128
+PACK = 4
+CH = 128
+NCH = S // CH
+LIST_ROWS = 16
+W1_SCALAR = 80
+E1_VECTOR = (2,)
+G1_VECTOR = ((0,2),(0,3))
+E2_VECTOR = ((2,0),(2,1),(2,2),(2,3))
+G2_VECTOR = ((0,2),(0,3))
+LAG = 3
+W3C_TAG = "z_bf1"
+W3S_TAG = "d_bf1"
+D_TAG = (0,1,0,0)
+T_TAG = (0,0,1,2)
+DB = 2
+TB = 4
+
+
+def tile_picked_rectwice_none_po_kernel(
+    tc, x_words, x_scales, w1, w2, w3_words, w3_scales, res, offs, n1, n2, out_0, out_1, out_2
+):
+    nc = tc.nc
+    with ExitStack() as ctx:
+        keep = ctx.enter_context(tc.tile_pool(name="keep", bufs=1))
+        psum = ctx.enter_context(tc.psum_pool(name="psum", bufs=1))
+
+        def sb(name, shape, dtype, tag=None):
+            return keep.tile(shape, dtype, name=name, tag=tag or name, align_bytes=64)
+
+        def cols(c):
+            return slice(c * CH, (c + 1) * CH)
+
+        def entries(lst, c):
+            return lst[:, c * CH // LIST_ROWS : (c + 1) * CH // LIST_ROWS]
+
+        def words_i32(dram):
+            return dram[0].rearrange("p n t -> p (n t)").bitcast(I32)
+
+        def by_fours(ap):
+            return ap.rearrange("p t (c i) -> p c t i", i=4)
+
+        def woven(ap):
+            return ap.rearrange("p (c i t) -> p c t i", i=4, t=PACK)
+
+        offs_t = sb("offs_t", [P, S // LIST_ROWS], U16)
+        n1_t = sb("n1_t", [P, S // LIST_ROWS], U16)
+        n2_t = sb("n2_t", [P, S // LIST_ROWS], U16)
+        xs_all = sb("xs_all", [P, T], U8)
+        xw_all = sb("xw_all", [P, T], U32)
+        w1_raw = sb("w1_raw", [P, PACK, H], F32)
+        w2_raw = sb("w2_raw", [P, PACK, H], F32)
+        w3w_raw = sb("w3w_raw", [P, N], U32)
+        w3s_raw = sb("w3s_raw", [P, N], U8)
+        res_t = sb("res_t", [P, PACK, S], F32)
+
+        nc.vector.memset(xs_all[:, : T // 2].bitcast(I32), 0)
+        nc.gpsimd.memset(xs_all[:, T // 2 :].bitcast(I32), 0)
+        nc.gpsimd.memset(w3s_raw[:].bitcast(I32), 0)
+
+        nc.sync.dma_start(offs_t[:], offs)
+        nc.sync.dma_start(w1_raw[:], w1.rearrange("(p j) c -> p j c", j=PACK))
+        for q in range(4):
+            nc.sync.dma_start(xs_all[32 * q : 32 * q + 4, :].bitcast(I32), x_scales[0, 4 * q : 4 * q + 4, :].bitcast(I32))
+        nc.sync.dma_start(xw_all[:].bitcast(I32), words_i32(x_words))
+        nc.sync.dma_start(n1_t[:], n1)
+        nc.sync.dma_start(w2_raw[:], w2.rearrange("(p j) c -> p j c", j=PACK))
+        nc.sync.dma_start(w3w_raw[:].bitcast(I32), words_i32(w3_words))
+        for q in range(4):
+            nc.sync.dma_start(w3s_raw[32 * q : 32 * q + 4, :].bitcast(I32), w3_scales[0, 4 * q : 4 * q + 4, :].bitcast(I32))
+        nc.sync.dma_start(n2_t[:], n2)
+        nc.sync.dma_start(res_t[:], res.rearrange("(p t) j -> p t j", t=PACK))
+
+        def dealt_views(raw, grouped, m0, m1):
+            src = raw[:].rearrange("p j (m t) -> p m j t", t=PACK)[:, m0:m1]
+            dst = grouped[:].rearrange("p (t m j) -> p m j t", t=PACK, j=PACK)[:, m0:m1]
+            return dst, src
+
+        def quantize(codes, scales, values):
+            nc.vector.quantize_mx(out=codes.bitcast(FP8X4), scales=scales, in_=values)
+
+        def product(bank, w_codes, w_scales, codes, scales):
+            for t in range(PACK):
+                nc.tensor.matmul_mx(
+                    out=bank[:, t, :],
+                    lhsT=w_codes[:, cols(t)].bitcast(FP8X4),
+                    lhsT_scale=w_scales[:, cols(t)],
+                    rhs=codes.bitcast(FP8X4),
+                    rhs_scale=scales,
+                    start=True,
+                    stop=True,
+                )
+
+        def product_t(bank, t, w_codes, w_scales, codes, scales):
+            nc.tensor.matmul_mx(
+                out=bank[:, t, :],
+                lhsT=w_codes[:, cols(t)].bitcast(FP8X4),
+                lhsT_scale=w_scales[:, cols(t)],
+                rhs=codes.bitcast(FP8X4),
+                rhs_scale=scales,
+                start=True,
+                stop=True,
+            )
+
+        def fetch(on_vector, dst, window, lst, j0, j1):
+            src = window[:].indirect(lst[:, j0 // LIST_ROWS : j1 // LIST_ROWS])
+            if on_vector:
+                nc.vector.tensor_copy(dst, src)
+            else:
+                nc.scalar.activation(dst, src, COPY)
+
+        def leave(on_vector, dst, src):
+            if on_vector:
+                nc.vector.tensor_copy(dst, src)
+            else:
+                nc.scalar.copy(dst, src)
+
+        w1_bf = sb("w1_bf", [P, PACK * H], BF16)
+        w1_c = sb("w1_c", [P, H], U32)
+        w1_s = sb("w1_s", [P, H], U8)
+        xs = sb("xs", [P, S], U8)
+        dst, src = dealt_views(w1_raw, w1_bf, 0, W1_SCALAR)
+        nc.scalar.activation(dst, src, COPY)
+        dst, src = dealt_views(w1_raw, w1_bf, W1_SCALAR, 128)
+        nc.vector.tensor_copy(dst, src)
+        nc.vector.tensor_copy(xs[:], xs_all[:].indirect(offs_t[:]))
+        quantize(w1_c[:], w1_s[:], w1_bf[:])
+
+        xw = sb("xw", [P, S], U32)
+        y_bank = [psum.tile([P, PACK, CH], F32, name="a%d" % c) for c in range(NCH)]
+        y_win = [sb("y_win%d" % t, [P, S], F32) for t in range(PACK)]
+        g1 = [sb("g1_%d" % c, [P, PACK, CH], F32) for c in range(NCH)]
+        for c in range(NCH):
+            nc.vector.tensor_copy(xw[:, cols(c)], xw_all[:].indirect(entries(offs_t, c)))
+        for c in range(NCH):
+            product(y_bank[c], w1_c, w1_s, xw[:, cols(c)], xs[:, cols(c)])
+            for t in range(PACK):
+                leave(c in E1_VECTOR, y_win[t][:, cols(c)], y_bank[c][:, t, :])
+        for c in range(NCH):
+            for t in range(PACK):
+                fetch((c, t) in G1_VECTOR, g1[c][:, t, :], y_win[t], n1_t, c * CH, (c + 1) * CH)
+
+        w2_bf = sb("w2_bf", [P, PACK * H], BF16)
+        w2_c = sb("w2_c", [P, H], U32)
+        w2_s = sb("w2_s", [P, H], U8)
+        for m0 in (0, 64):
+            dst, src = dealt_views(w2_raw, w2_bf, m0, m0 + 64)
+            nc.vector.tensor_copy(dst, src)
+        quantize(w2_c[:], w2_s[:], w2_bf[:])
+
+        h_bank = [psum.tile([P, PACK, CH], F32, name="b%d" % c) for c in range(NCH)]
+        h_win = [sb("h_win%d" % t, [P, S], F32) for t in range(PACK)]
+        z_c = sb("z_c", [P, S], U32)
+        z_s = sb("z_s", [P, S], U8)
+        for c in range(NCH):
+            d_bf = sb("d_bf%d" % (c % DB), [P, PACK * CH], BF16)
+            z_bf = sb("z_bf%d" % (c % DB), [P, PACK * CH], BF16)
+            nc.vector.tensor_tensor(woven(d_bf[:]), by_fours(y_bank[c][:]), by_fours(g1[c][:]), ALU.subtract)
+            nc.vector.tensor_scalar_max(z_bf[:], d_bf[:], 0.0)
+            quantize(z_c[:, cols(c)], z_s[:, cols(c)], z_bf[:])
+            product(h_bank[c], w2_c, w2_s, z_c[:, cols(c)], z_s[:, cols(c)])
+
+        w3_c = sb("w3_c", [P, N], U32, W3C_TAG)
+        w3_s = sb("w3_s", [P, N], U8, W3S_TAG)
+        nc.vector.tensor_copy(
+            w3_c[:].bitcast(I32).rearrange("p (t c i) -> p c t i", t=PACK, i=4),
+            w3w_raw[:].bitcast(I32).rearrange("p (c i t) -> p c t i", t=PACK, i=4),
+        )
+        nc.vector.tensor_copy(
+            w3_s[:].rearrange("p (t m) -> p t m", t=PACK),
+            w3s_raw[:].rearrange("p (m t) -> p t m", t=PACK),
+        )
+
+        for c in range(NCH):
+            for t in range(PACK):
+                leave((c, t) in E2_VECTOR, h_win[t][:, cols(c)], h_bank[c][:, t, :])
+
+        g2 = [sb("g2_%d" % c, [P, PACK, CH], F32) for c in range(NCH)]
+        z2_c = sb("z2_c", [P, S], U32)
+        z2_s = sb("z2_s", [P, S], U8)
+        o_c = sb("o_c", [P, S], U32)
+        o_s = sb("o_s", [P, S], U8)
+        out_rows = out_0.rearrange("(p t) j -> p t j", t=PACK)
+        for c in range(NCH):
+            for t in range(PACK):
+                fetch((c, t) in G2_VECTOR, g2[c][:, t, :], h_win[t], n2_t, c * CH, (c + 1) * CH)
+        o_bank = {}
+
+        def second_step(c):
+            top = sb("top%d" % (c % TB), [P, PACK * CH], F32)
+            z2_bf = sb("z2_bf%d" % c, [P, PACK * CH], BF16)
+            nc.vector.tensor_tensor(woven(top[:]), by_fours(h_bank[c][:]), by_fours(g2[c][:]), ALU.max)
+            nc.vector.scalar_tensor_tensor(
+                z2_bf[:].rearrange("p (j t) -> p j t", t=PACK),
+                h_bank[c][:].rearrange("p t j -> p j t"),
+                -1.25,
+                top[:].rearrange("p (j t) -> p j t", t=PACK),
+                ALU.mult,
+                ALU.add,
+            )
+            quantize(z2_c[:, cols(c)], z2_s[:, cols(c)], z2_bf[:])
+            o_bank[c] = psum.tile([P, PACK, CH], F32, name="a%d" % c)
+            product(o_bank[c], w3_c, w3_s, z2_c[:, cols(c)], z2_s[:, cols(c)])
+
+        def hand_out(c):
+            o = sb("o%d" % c, [P, PACK, CH], F32)
+            o_bf = sb("o_bf%d" % c, [P, PACK * CH], BF16)
+            nc.vector.tensor_tensor(o[:], o_bank[c][:], res_t[:, :, cols(c)], ALU.add)
+            nc.sync.dma_start(out_rows[:, :, cols(c)], o[:])
+            leave(c == NCH - 1, woven(o_bf[:]), by_fours(o[:]))
+            quantize(o_c[:, cols(c)], o_s[:, cols(c)], o_bf[:])
+            if c >= NCH - 2:
+                done = slice(0, (NCH - 1) * CH) if c == NCH - 2 else cols(c)
+                nc.sync.dma_start(words_i32(out_1)[:, done], o_c[:, done].bitcast(I32))
+
+        for c in range(NCH + LAG):
+            if c < NCH:
+                second_step(c)
+            if c >= LAG:
+                hand_out(c - LAG)
+        for q in range(4):
+            eng = nc.scalar if q % 2 else nc.sync
+            eng.dma_start(out_2[0, 4 * q : 4 * q + 4, :].bitcast(I32), o_s[32 * q : 32 * q + 4, :].bitcast(I32))

@@ -13,6 +13,7 @@ U16 = mybir.dt.uint16
 U8 = mybir.dt.uint8
 FP8X4 = mybir.dt.float8_e4m3fn_x4
 ALU = mybir.AluOpType
+RELU = mybir.ActivationFunctionType.Relu
 COPY = mybir.ActivationFunctionType.Copy
 
 P = 128
@@ -21,17 +22,36 @@ CH = 128
 NCH = S // CH
 LIST_ROWS = 16
 W1_SCALAR = 80
-E1_VECTOR = (2,)
+E1_VECTOR = (1,)
 G1_VECTOR = ((0,2),(0,3))
-E2_VECTOR = ((2,0),(2,1),(2,2),(2,3))
-G2_VECTOR = ((0,2),(0,3))
-LAG = 3
-W3C_TAG = "z_bf1"
-W3S_TAG = "d_bf1"
+E2_VECTOR = ((3,0),(3,1),(3,2),(3,3))
+G2_VECTOR = ((0,2),(0,3),(1,3))
+LAG = 2
+W3C_TAG = "z_bf3"
+W3S_TAG = "d_bf3"
 D_TAG = (0,1,0,0)
 T_TAG = (0,0,1,2)
-DB = 2
 TB = 4
+MM1_ORDER = ((0,0),(1,0),(0,1),(1,1),(2,0),(2,1),(3,0),(3,1))
+G1_ORDER = ((0,0),(0,1),(0,2),(0,3),(1,0),(1,1),(1,2),(1,3))
+W2_STEP = 64
+W2_G = 1
+R_SCALAR = ()
+PIECES = ((0,2),(2,3),(3,4))
+G1_TAG = (0,0,1)
+D1_TAG = (0,1,2)
+ADD_G = ()
+ADD_STEP = 2
+DB = 4
+SPREAD1 = 1
+SPREAD2 = 1
+S1_VECTOR = (1,2,3)
+S2_VECTOR = (0,1,2,3)
+W2_BEFORE = 1
+W2_V = ((0,64),(64,128))
+W2_S = 0
+W2_S_AT = 9
+HALF = 256
 
 
 def tile_picked_rectwice_none_po_kernel(
@@ -149,19 +169,39 @@ def tile_picked_rectwice_none_po_kernel(
         g1 = [sb("g1_%d" % c, [P, PACK, CH], F32) for c in range(NCH)]
         for c in range(NCH):
             nc.vector.tensor_copy(xw[:, cols(c)], xw_all[:].indirect(entries(offs_t, c)))
-        for c in range(NCH):
-            product(y_bank[c], w1_c, w1_s, xw[:, cols(c)], xs[:, cols(c)])
+        def spread(tag, win, on_vector, w_codes, w_scales, codes, scales):
             for t in range(PACK):
-                leave(c in E1_VECTOR, y_win[t][:, cols(c)], y_bank[c][:, t, :])
+                bank = psum.tile([P, 1, CH], F32, name="%s%d" % (tag, t))
+                nc.tensor.matmul_mx(
+                    out=bank[:, 0, :],
+                    lhsT=w_codes[:, cols(t)].bitcast(FP8X4),
+                    lhsT_scale=w_scales[:, cols(t)],
+                    rhs=codes.bitcast(FP8X4),
+                    rhs_scale=scales,
+                    start=True,
+                    stop=True,
+                )
+                leave(t in on_vector, win[t][:, cols(NCH - 1)], bank[:, 0, :])
+
         for c in range(NCH):
+            if c == NCH - 1 and SPREAD1:
+                spread("b", y_win, S1_VECTOR, w1_c, w1_s, xw[:, cols(c)], xs[:, cols(c)])
+            product(y_bank[c], w1_c, w1_s, xw[:, cols(c)], xs[:, cols(c)])
+            if c < NCH - 1 or not SPREAD1:
+                for t in range(PACK):
+                    leave(c in E1_VECTOR, y_win[t][:, cols(c)], y_bank[c][:, t, :])
+        w2_bf = sb("w2_bf", [P, PACK * H], BF16)
+        for c in range(NCH):
+            if c == W2_S_AT:
+                dst, src = dealt_views(w2_raw, w2_bf, 0, W2_S)
+                nc.scalar.copy(dst, src)
             for t in range(PACK):
                 fetch((c, t) in G1_VECTOR, g1[c][:, t, :], y_win[t], n1_t, c * CH, (c + 1) * CH)
 
-        w2_bf = sb("w2_bf", [P, PACK * H], BF16)
         w2_c = sb("w2_c", [P, H], U32)
         w2_s = sb("w2_s", [P, H], U8)
-        for m0 in (0, 64):
-            dst, src = dealt_views(w2_raw, w2_bf, m0, m0 + 64)
+        for m0, m1 in W2_V:
+            dst, src = dealt_views(w2_raw, w2_bf, m0, m1)
             nc.vector.tensor_copy(dst, src)
         quantize(w2_c[:], w2_s[:], w2_bf[:])
 
@@ -173,8 +213,13 @@ def tile_picked_rectwice_none_po_kernel(
             d_bf = sb("d_bf%d" % (c % DB), [P, PACK * CH], BF16)
             z_bf = sb("z_bf%d" % (c % DB), [P, PACK * CH], BF16)
             nc.vector.tensor_tensor(woven(d_bf[:]), by_fours(y_bank[c][:]), by_fours(g1[c][:]), ALU.subtract)
-            nc.vector.tensor_scalar_max(z_bf[:], d_bf[:], 0.0)
+            if c in R_SCALAR:
+                nc.scalar.activation(z_bf[:], d_bf[:], RELU)
+            else:
+                nc.vector.tensor_scalar_max(z_bf[:], d_bf[:], 0.0)
             quantize(z_c[:, cols(c)], z_s[:, cols(c)], z_bf[:])
+            if c == NCH - 1 and SPREAD2:
+                spread("a", h_win, S2_VECTOR, w2_c, w2_s, z_c[:, cols(c)], z_s[:, cols(c)])
             product(h_bank[c], w2_c, w2_s, z_c[:, cols(c)], z_s[:, cols(c)])
 
         w3_c = sb("w3_c", [P, N], U32, W3C_TAG)
@@ -188,7 +233,7 @@ def tile_picked_rectwice_none_po_kernel(
             w3s_raw[:].rearrange("p (m t) -> p t m", t=PACK),
         )
 
-        for c in range(NCH):
+        for c in range(NCH - SPREAD2):
             for t in range(PACK):
                 leave((c, t) in E2_VECTOR, h_win[t][:, cols(c)], h_bank[c][:, t, :])
 
@@ -226,9 +271,10 @@ def tile_picked_rectwice_none_po_kernel(
             nc.sync.dma_start(out_rows[:, :, cols(c)], o[:])
             leave(c == NCH - 1, woven(o_bf[:]), by_fours(o[:]))
             quantize(o_c[:, cols(c)], o_s[:, cols(c)], o_bf[:])
-            if c >= NCH - 2:
-                done = slice(0, (NCH - 1) * CH) if c == NCH - 2 else cols(c)
-                nc.sync.dma_start(words_i32(out_1)[:, done], o_c[:, done].bitcast(I32))
+            if c % 2:
+                done = slice((c - 1) * CH, (c + 1) * CH)
+                eng = nc.scalar if c == NCH - 1 else nc.sync
+                eng.dma_start(words_i32(out_1)[:, done], o_c[:, done].bitcast(I32))
 
         for c in range(NCH + LAG):
             if c < NCH:

@@ -22,11 +22,11 @@ CH = 128
 NCH = S // CH
 LIST_ROWS = 16
 W1_SCALAR = 80
-E1_VECTOR = (1,)
+E1_VECTOR = ()
 G1_VECTOR = ((0,2),(0,3))
-E2_VECTOR = ((3,0),(3,1),(3,2),(3,3))
-G2_VECTOR = ((0,2),(0,3),(1,3))
-LAG = 2
+E2_VECTOR = ()
+G2_VECTOR = ((0,2),(0,3))
+LAG = 3
 W3C_TAG = "z_bf3"
 W3S_TAG = "d_bf3"
 D_TAG = (0,1,0,0)
@@ -43,7 +43,7 @@ D1_TAG = (0,1,2)
 ADD_G = ()
 ADD_STEP = 2
 DB = 4
-SPREAD1 = 1
+SPREAD1 = 0
 SPREAD2 = 1
 S1_VECTOR = (1,2,3)
 S2_VECTOR = (0,1,2,3)
@@ -51,6 +51,13 @@ W2_BEFORE = 1
 W2_V = ((0,64),(64,128))
 W2_S = 0
 W2_S_AT = 9
+XG = ((0,128),(128,256),(256,384),(384,512))
+Q1 = ((0,1),(1,2),(2,3),(3,4))
+QO = ((0,2),(2,3),(3,4))
+FLAT1 = ()
+CAST_V = (3,)
+WEAVE_S = ()
+W3_V = 1
 HALF = 256
 
 
@@ -95,8 +102,8 @@ def tile_picked_rectwice_none_po_kernel(
         nc.gpsimd.memset(xs_all[:, T // 2 :].bitcast(I32), 0)
         nc.gpsimd.memset(w3s_raw[:].bitcast(I32), 0)
 
-        nc.sync.dma_start(offs_t[:], offs)
         nc.sync.dma_start(w1_raw[:], w1.rearrange("(p j) c -> p j c", j=PACK))
+        nc.sync.dma_start(offs_t[:], offs)
         for q in range(4):
             nc.sync.dma_start(xs_all[32 * q : 32 * q + 4, :].bitcast(I32), x_scales[0, 4 * q : 4 * q + 4, :].bitcast(I32))
         nc.sync.dma_start(xw_all[:].bitcast(I32), words_i32(x_words))
@@ -109,8 +116,8 @@ def tile_picked_rectwice_none_po_kernel(
         nc.sync.dma_start(res_t[:], res.rearrange("(p t) j -> p t j", t=PACK))
 
         def dealt_views(raw, grouped, m0, m1):
-            src = raw[:].rearrange("p j (m t) -> p m j t", t=PACK)[:, m0:m1]
-            dst = grouped[:].rearrange("p (t m j) -> p m j t", t=PACK, j=PACK)[:, m0:m1]
+            src = raw[:].rearrange("p j (m t) -> p m t j", t=PACK)[:, m0:m1]
+            dst = grouped[:].rearrange("p (t m j) -> p m t j", t=PACK, j=PACK)[:, m0:m1]
             return dst, src
 
         def quantize(codes, scales, values):
@@ -167,8 +174,8 @@ def tile_picked_rectwice_none_po_kernel(
         y_bank = [psum.tile([P, PACK, CH], F32, name="a%d" % c) for c in range(NCH)]
         y_win = [sb("y_win%d" % t, [P, S], F32) for t in range(PACK)]
         g1 = [sb("g1_%d" % c, [P, PACK, CH], F32) for c in range(NCH)]
-        for c in range(NCH):
-            nc.vector.tensor_copy(xw[:, cols(c)], xw_all[:].indirect(entries(offs_t, c)))
+        for j0, j1 in XG:
+            nc.vector.tensor_copy(xw[:, j0:j1], xw_all[:].indirect(offs_t[:, j0 // LIST_ROWS : j1 // LIST_ROWS]))
         def spread(tag, win, on_vector, w_codes, w_scales, codes, scales):
             for t in range(PACK):
                 bank = psum.tile([P, 1, CH], F32, name="%s%d" % (tag, t))
@@ -209,18 +216,28 @@ def tile_picked_rectwice_none_po_kernel(
         h_win = [sb("h_win%d" % t, [P, S], F32) for t in range(PACK)]
         z_c = sb("z_c", [P, S], U32)
         z_s = sb("z_s", [P, S], U8)
-        for c in range(NCH):
-            d_bf = sb("d_bf%d" % (c % DB), [P, PACK * CH], BF16)
-            z_bf = sb("z_bf%d" % (c % DB), [P, PACK * CH], BF16)
-            nc.vector.tensor_tensor(woven(d_bf[:]), by_fours(y_bank[c][:]), by_fours(g1[c][:]), ALU.subtract)
-            if c in R_SCALAR:
-                nc.scalar.activation(z_bf[:], d_bf[:], RELU)
-            else:
+        for c0, c1 in Q1:
+            d_bf = sb("d_bf%d" % c0, [P, (c1 - c0) * PACK * CH], BF16)
+            z_bf = sb("z_bf%d" % c0, [P, (c1 - c0) * PACK * CH], BF16)
+            for c in range(c0, c1):
+                part = slice((c - c0) * PACK * CH, (c - c0 + 1) * PACK * CH)
+                if c in FLAT1:
+                    d32 = sb("d32_%d" % c, [P, PACK, CH], F32)
+                    nc.vector.tensor_tensor(d32[:], y_bank[c][:], g1[c][:], ALU.subtract)
+                    if c in R_SCALAR:
+                        nc.scalar.activation(woven(z_bf[:, part]), by_fours(d32[:]), RELU)
+                    else:
+                        nc.vector.tensor_scalar_max(woven(z_bf[:, part]), by_fours(d32[:]), 0.0)
+                else:
+                    nc.vector.tensor_tensor(woven(d_bf[:, part]), by_fours(y_bank[c][:]), by_fours(g1[c][:]), ALU.subtract)
+            if c0 not in FLAT1:
                 nc.vector.tensor_scalar_max(z_bf[:], d_bf[:], 0.0)
-            quantize(z_c[:, cols(c)], z_s[:, cols(c)], z_bf[:])
-            if c == NCH - 1 and SPREAD2:
-                spread("a", h_win, S2_VECTOR, w2_c, w2_s, z_c[:, cols(c)], z_s[:, cols(c)])
-            product(h_bank[c], w2_c, w2_s, z_c[:, cols(c)], z_s[:, cols(c)])
+            both = slice(c0 * CH, c1 * CH)
+            quantize(z_c[:, both], z_s[:, both], z_bf[:])
+            for c in range(c0, c1):
+                if c == NCH - 1 and SPREAD2:
+                    spread("a", h_win, S2_VECTOR, w2_c, w2_s, z_c[:, cols(c)], z_s[:, cols(c)])
+                product(h_bank[c], w2_c, w2_s, z_c[:, cols(c)], z_s[:, cols(c)])
 
         w3_c = sb("w3_c", [P, N], U32, W3C_TAG)
         w3_s = sb("w3_s", [P, N], U8, W3S_TAG)
@@ -247,34 +264,42 @@ def tile_picked_rectwice_none_po_kernel(
             for t in range(PACK):
                 fetch((c, t) in G2_VECTOR, g2[c][:, t, :], h_win[t], n2_t, c * CH, (c + 1) * CH)
         o_bank = {}
+        o_bf = sb("o_bf", [P, PACK * S], BF16)
 
         def second_step(c):
             top = sb("top%d" % (c % TB), [P, PACK * CH], F32)
             z2_bf = sb("z2_bf%d" % c, [P, PACK * CH], BF16)
-            nc.vector.tensor_tensor(woven(top[:]), by_fours(h_bank[c][:]), by_fours(g2[c][:]), ALU.max)
-            nc.vector.scalar_tensor_tensor(
-                z2_bf[:].rearrange("p (j t) -> p j t", t=PACK),
-                h_bank[c][:].rearrange("p t j -> p j t"),
-                -1.25,
-                top[:].rearrange("p (j t) -> p j t", t=PACK),
-                ALU.mult,
-                ALU.add,
-            )
+            if c in WEAVE_S:
+                flat = sb("flat%d" % c, [P, PACK, CH], F32)
+                tv = top[:].rearrange("p (t j) -> p t j", t=PACK)
+                nc.vector.tensor_tensor(tv, h_bank[c][:], g2[c][:], ALU.max)
+                nc.vector.scalar_tensor_tensor(flat[:], h_bank[c][:], -1.25, tv, ALU.mult, ALU.add)
+                nc.scalar.copy(woven(z2_bf[:]), by_fours(flat[:]))
+            else:
+                nc.vector.tensor_tensor(woven(top[:]), by_fours(h_bank[c][:]), by_fours(g2[c][:]), ALU.max)
+                nc.vector.scalar_tensor_tensor(
+                    z2_bf[:].rearrange("p (j t) -> p j t", t=PACK),
+                    h_bank[c][:].rearrange("p t j -> p j t"),
+                    -1.25,
+                    top[:].rearrange("p (j t) -> p j t", t=PACK),
+                    ALU.mult,
+                    ALU.add,
+                )
             quantize(z2_c[:, cols(c)], z2_s[:, cols(c)], z2_bf[:])
             o_bank[c] = psum.tile([P, PACK, CH], F32, name="a%d" % c)
             product(o_bank[c], w3_c, w3_s, z2_c[:, cols(c)], z2_s[:, cols(c)])
 
         def hand_out(c):
             o = sb("o%d" % c, [P, PACK, CH], F32)
-            o_bf = sb("o_bf%d" % c, [P, PACK * CH], BF16)
             nc.vector.tensor_tensor(o[:], o_bank[c][:], res_t[:, :, cols(c)], ALU.add)
             nc.sync.dma_start(out_rows[:, :, cols(c)], o[:])
-            leave(c == NCH - 1, woven(o_bf[:]), by_fours(o[:]))
-            quantize(o_c[:, cols(c)], o_s[:, cols(c)], o_bf[:])
-            if c % 2:
-                done = slice((c - 1) * CH, (c + 1) * CH)
-                eng = nc.scalar if c == NCH - 1 else nc.sync
-                eng.dma_start(words_i32(out_1)[:, done], o_c[:, done].bitcast(I32))
+            leave(c in CAST_V, woven(o_bf[:, c * PACK * CH : (c + 1) * PACK * CH]), by_fours(o[:]))
+            for c0, c1 in QO:
+                if c == c1 - 1:
+                    quantize(o_c[:, c0 * CH : c1 * CH], o_s[:, c0 * CH : c1 * CH], o_bf[:, c0 * PACK * CH : c1 * PACK * CH])
+            if c >= NCH - 2:
+                done = slice(0, (NCH - 1) * CH) if c == NCH - 2 else cols(c)
+                nc.sync.dma_start(words_i32(out_1)[:, done], o_c[:, done].bitcast(I32))
 
         for c in range(NCH + LAG):
             if c < NCH:

from contextlib import ExitStack

import concourse.mybir as mybir

K, T, S, N, H = 512, 2048, 512, 512, 512
FLOPS = 3 * 2 * 512 * 512 * 512

F32 = mybir.dt.float32
BF16 = mybir.dt.bfloat16
I32 = mybir.dt.int32
U32 = mybir.dt.uint32
U16 = mybir.dt.uint16
U8 = mybir.dt.uint8
FP8X4 = mybir.dt.float8_e4m3fn_x4
ALU = mybir.AluOpType
RELU = mybir.ActivationFunctionType.Relu
COPY = mybir.ActivationFunctionType.Copy

P = 128
PACK = 4
CH = 128
NCH = S // CH
LIST_ROWS = 16
W1_SCALAR = 80
E1_VECTOR = ()
G1_VECTOR = ((0,2),(0,3))
E2_VECTOR = ()
G2_VECTOR = ((0,2),(0,3))
LAG = 3
W3C_TAG = "z_bf3"
W3S_TAG = "d_bf3"
D_TAG = (0,1,0,0)
T_TAG = (0,0,1,2)
TB = 4
MM1_ORDER = ((0,0),(1,0),(0,1),(1,1),(2,0),(2,1),(3,0),(3,1))
G1_ORDER = ((0,0),(0,1),(0,2),(0,3),(1,0),(1,1),(1,2),(1,3))
W2_STEP = 64
W2_G = 1
R_SCALAR = ()
PIECES = ((0,2),(2,3),(3,4))
G1_TAG = (0,0,1)
D1_TAG = (0,1,2)
ADD_G = ()
ADD_STEP = 2
DB = 4
SPREAD1 = 0
SPREAD2 = 1
S1_VECTOR = (1,2,3)
S2_VECTOR = (0,1,2,3)
W2_BEFORE = 1
W2_V = ((0,64),(64,128))
W2_S = 0
W2_S_AT = 9
XG = ((0,128),(128,256),(256,384),(384,512))
Q1 = ((0,1),(1,2),(2,3),(3,4))
QO = ((0,2),(2,3),(3,4))
FLAT1 = ()
CAST_V = (3,)
WEAVE_S = ()
W3_V = 1
HALF = 256


def tile_picked_rectwice_none_po_kernel(
    tc, x_words, x_scales, w1, w2, w3_words, w3_scales, res, offs, n1, n2, out_0, out_1, out_2
):
    nc = tc.nc
    with ExitStack() as ctx:
        keep = ctx.enter_context(tc.tile_pool(name="keep", bufs=1))
        psum = ctx.enter_context(tc.psum_pool(name="psum", bufs=1))

        def sb(name, shape, dtype, tag=None):
            return keep.tile(shape, dtype, name=name, tag=tag or name, align_bytes=64)

        def cols(c):
            return slice(c * CH, (c + 1) * CH)

        def entries(lst, c):
            return lst[:, c * CH // LIST_ROWS : (c + 1) * CH // LIST_ROWS]

        def words_i32(dram):
            return dram[0].rearrange("p n t -> p (n t)").bitcast(I32)

        def by_fours(ap):
            return ap.rearrange("p t (c i) -> p c t i", i=4)

        def woven(ap):
            return ap.rearrange("p (c i t) -> p c t i", i=4, t=PACK)

        offs_t = sb("offs_t", [P, S // LIST_ROWS], U16)
        n1_t = sb("n1_t", [P, S // LIST_ROWS], U16)
        n2_t = sb("n2_t", [P, S // LIST_ROWS], U16)
        xs_all = sb("xs_all", [P, T], U8)
        xw_all = sb("xw_all", [P, T], U32)
        w1_raw = sb("w1_raw", [P, PACK, H], F32)
        w2_raw = sb("w2_raw", [P, PACK, H], F32)
        w3w_raw = sb("w3w_raw", [P, N], U32)
        w3s_raw = sb("w3s_raw", [P, N], U8)
        res_t = sb("res_t", [P, PACK, S], F32)

        nc.vector.memset(xs_all[:, : T // 2].bitcast(I32), 0)
        nc.gpsimd.memset(xs_all[:, T // 2 :].bitcast(I32), 0)
        nc.gpsimd.memset(w3s_raw[:].bitcast(I32), 0)

        nc.sync.dma_start(w1_raw[:], w1.rearrange("(p j) c -> p j c", j=PACK))
        nc.sync.dma_start(offs_t[:], offs)
        for q in range(4):
            nc.sync.dma_start(xs_all[32 * q : 32 * q + 4, :].bitcast(I32), x_scales[0, 4 * q : 4 * q + 4, :].bitcast(I32))
        nc.sync.dma_start(xw_all[:].bitcast(I32), words_i32(x_words))
        nc.sync.dma_start(n1_t[:], n1)
        nc.sync.dma_start(w2_raw[:], w2.rearrange("(p j) c -> p j c", j=PACK))
        nc.sync.dma_start(w3w_raw[:].bitcast(I32), words_i32(w3_words))
        for q in range(4):
            nc.sync.dma_start(w3s_raw[32 * q : 32 * q + 4, :].bitcast(I32), w3_scales[0, 4 * q : 4 * q + 4, :].bitcast(I32))
        nc.sync.dma_start(n2_t[:], n2)
        nc.sync.dma_start(res_t[:], res.rearrange("(p t) j -> p t j", t=PACK))

        def dealt_views(raw, grouped, m0, m1):
            src = raw[:].rearrange("p j (m t) -> p m t j", t=PACK)[:, m0:m1]
            dst = grouped[:].rearrange("p (t m j) -> p m t j", t=PACK, j=PACK)[:, m0:m1]
            return dst, src

        def quantize(codes, scales, values):
            nc.vector.quantize_mx(out=codes.bitcast(FP8X4), scales=scales, in_=values)

        def product(bank, w_codes, w_scales, codes, scales):
            for t in range(PACK):
                nc.tensor.matmul_mx(
                    out=bank[:, t, :],
                    lhsT=w_codes[:, cols(t)].bitcast(FP8X4),
                    lhsT_scale=w_scales[:, cols(t)],
                    rhs=codes.bitcast(FP8X4),
                    rhs_scale=scales,
                    start=True,
                    stop=True,
                )

        def product_t(bank, t, w_codes, w_scales, codes, scales):
            nc.tensor.matmul_mx(
                out=bank[:, t, :],
                lhsT=w_codes[:, cols(t)].bitcast(FP8X4),
                lhsT_scale=w_scales[:, cols(t)],
                rhs=codes.bitcast(FP8X4),
                rhs_scale=scales,
                start=True,
                stop=True,
            )

        def fetch(on_vector, dst, window, lst, j0, j1):
            src = window[:].indirect(lst[:, j0 // LIST_ROWS : j1 // LIST_ROWS])
            if on_vector:
                nc.vector.tensor_copy(dst, src)
            else:
                nc.scalar.activation(dst, src, COPY)

        def leave(on_vector, dst, src):
            if on_vector:
                nc.vector.tensor_copy(dst, src)
            else:
                nc.scalar.copy(dst, src)

        w1_bf = sb("w1_bf", [P, PACK * H], BF16)
        w1_c = sb("w1_c", [P, H], U32)
        w1_s = sb("w1_s", [P, H], U8)
        xs = sb("xs", [P, S], U8)
        dst, src = dealt_views(w1_raw, w1_bf, 0, W1_SCALAR)
        nc.scalar.activation(dst, src, COPY)
        dst, src = dealt_views(w1_raw, w1_bf, W1_SCALAR, 128)
        nc.vector.tensor_copy(dst, src)
        nc.vector.tensor_copy(xs[:], xs_all[:].indirect(offs_t[:]))
        quantize(w1_c[:], w1_s[:], w1_bf[:])

        xw = sb("xw", [P, S], U32)
        y_bank = [psum.tile([P, PACK, CH], F32, name="a%d" % c) for c in range(NCH)]
        y_win = [sb("y_win%d" % t, [P, S], F32) for t in range(PACK)]
        g1 = [sb("g1_%d" % c, [P, PACK, CH], F32) for c in range(NCH)]
        for j0, j1 in XG:
            nc.vector.tensor_copy(xw[:, j0:j1], xw_all[:].indirect(offs_t[:, j0 // LIST_ROWS : j1 // LIST_ROWS]))
        def spread(tag, win, on_vector, w_codes, w_scales, codes, scales):
            for t in range(PACK):
                bank = psum.tile([P, 1, CH], F32, name="%s%d" % (tag, t))
                nc.tensor.matmul_mx(
                    out=bank[:, 0, :],
                    lhsT=w_codes[:, cols(t)].bitcast(FP8X4),
                    lhsT_scale=w_scales[:, cols(t)],
                    rhs=codes.bitcast(FP8X4),
                    rhs_scale=scales,
                    start=True,
                    stop=True,
                )
                leave(t in on_vector, win[t][:, cols(NCH - 1)], bank[:, 0, :])

        for c in range(NCH):
            if c == NCH - 1 and SPREAD1:
                spread("b", y_win, S1_VECTOR, w1_c, w1_s, xw[:, cols(c)], xs[:, cols(c)])
            product(y_bank[c], w1_c, w1_s, xw[:, cols(c)], xs[:, cols(c)])
            if c < NCH - 1 or not SPREAD1:
                for t in range(PACK):
                    leave(c in E1_VECTOR, y_win[t][:, cols(c)], y_bank[c][:, t, :])
        w2_bf = sb("w2_bf", [P, PACK * H], BF16)
        for c in range(NCH):
            if c == W2_S_AT:
                dst, src = dealt_views(w2_raw, w2_bf, 0, W2_S)
                nc.scalar.copy(dst, src)
            for t in range(PACK):
                fetch((c, t) in G1_VECTOR, g1[c][:, t, :], y_win[t], n1_t, c * CH, (c + 1) * CH)

        w2_c = sb("w2_c", [P, H], U32)
        w2_s = sb("w2_s", [P, H], U8)
        for m0, m1 in W2_V:
            dst, src = dealt_views(w2_raw, w2_bf, m0, m1)
            nc.vector.tensor_copy(dst, src)
        quantize(w2_c[:], w2_s[:], w2_bf[:])

        h_bank = [psum.tile([P, PACK, CH], F32, name="b%d" % c) for c in range(NCH)]
        h_win = [sb("h_win%d" % t, [P, S], F32) for t in range(PACK)]
        z_c = sb("z_c", [P, S], U32)
        z_s = sb("z_s", [P, S], U8)
        for c0, c1 in Q1:
            d_bf = sb("d_bf%d" % c0, [P, (c1 - c0) * PACK * CH], BF16)
            z_bf = sb("z_bf%d" % c0, [P, (c1 - c0) * PACK * CH], BF16)
            for c in range(c0, c1):
                part = slice((c - c0) * PACK * CH, (c - c0 + 1) * PACK * CH)
                if c in FLAT1:
                    d32 = sb("d32_%d" % c, [P, PACK, CH], F32)
                    nc.vector.tensor_tensor(d32[:], y_bank[c][:], g1[c][:], ALU.subtract)
                    if c in R_SCALAR:
                        nc.scalar.activation(woven(z_bf[:, part]), by_fours(d32[:]), RELU)
                    else:
                        nc.vector.tensor_scalar_max(woven(z_bf[:, part]), by_fours(d32[:]), 0.0)
                else:
                    nc.vector.tensor_tensor(woven(d_bf[:, part]), by_fours(y_bank[c][:]), by_fours(g1[c][:]), ALU.subtract)
            if c0 not in FLAT1:
                nc.vector.tensor_scalar_max(z_bf[:], d_bf[:], 0.0)
            both = slice(c0 * CH, c1 * CH)
            quantize(z_c[:, both], z_s[:, both], z_bf[:])
            for c in range(c0, c1):
                if c == NCH - 1 and SPREAD2:
                    spread("a", h_win, S2_VECTOR, w2_c, w2_s, z_c[:, cols(c)], z_s[:, cols(c)])
                product(h_bank[c], w2_c, w2_s, z_c[:, cols(c)], z_s[:, cols(c)])

        w3_c = sb("w3_c", [P, N], U32, W3C_TAG)
        w3_s = sb("w3_s", [P, N], U8, W3S_TAG)
        nc.vector.tensor_copy(
            w3_c[:].bitcast(I32).rearrange("p (t c i) -> p c t i", t=PACK, i=4),
            w3w_raw[:].bitcast(I32).rearrange("p (c i t) -> p c t i", t=PACK, i=4),
        )
        nc.vector.tensor_copy(
            w3_s[:].rearrange("p (t m) -> p t m", t=PACK),
            w3s_raw[:].rearrange("p (m t) -> p t m", t=PACK),
        )

        for c in range(NCH - SPREAD2):
            for t in range(PACK):
                leave((c, t) in E2_VECTOR, h_win[t][:, cols(c)], h_bank[c][:, t, :])

        g2 = [sb("g2_%d" % c, [P, PACK, CH], F32) for c in range(NCH)]
        z2_c = sb("z2_c", [P, S], U32)
        z2_s = sb("z2_s", [P, S], U8)
        o_c = sb("o_c", [P, S], U32)
        o_s = sb("o_s", [P, S], U8)
        out_rows = out_0.rearrange("(p t) j -> p t j", t=PACK)
        for c in range(NCH):
            for t in range(PACK):
                fetch((c, t) in G2_VECTOR, g2[c][:, t, :], h_win[t], n2_t, c * CH, (c + 1) * CH)
        o_bank = {}
        o_bf = sb("o_bf", [P, PACK * S], BF16)

        def second_step(c):
            top = sb("top%d" % (c % TB), [P, PACK * CH], F32)
            z2_bf = sb("z2_bf%d" % c, [P, PACK * CH], BF16)
            if c in WEAVE_S:
                flat = sb("flat%d" % c, [P, PACK, CH], F32)
                tv = top[:].rearrange("p (t j) -> p t j", t=PACK)
                nc.vector.tensor_tensor(tv, h_bank[c][:], g2[c][:], ALU.max)
                nc.vector.scalar_tensor_tensor(flat[:], h_bank[c][:], -1.25, tv, ALU.mult, ALU.add)
                nc.scalar.copy(woven(z2_bf[:]), by_fours(flat[:]))
            else:
                nc.vector.tensor_tensor(woven(top[:]), by_fours(h_bank[c][:]), by_fours(g2[c][:]), ALU.max)
                nc.vector.scalar_tensor_tensor(
                    z2_bf[:].rearrange("p (j t) -> p j t", t=PACK),
                    h_bank[c][:].rearrange("p t j -> p j t"),
                    -1.25,
                    top[:].rearrange("p (j t) -> p j t", t=PACK),
                    ALU.mult,
                    ALU.add,
                )
            quantize(z2_c[:, cols(c)], z2_s[:, cols(c)], z2_bf[:])
            o_bank[c] = psum.tile([P, PACK, CH], F32, name="a%d" % c)
            product(o_bank[c], w3_c, w3_s, z2_c[:, cols(c)], z2_s[:, cols(c)])

        def hand_out(c):
            o = sb("o%d" % c, [P, PACK, CH], F32)
            nc.vector.tensor_tensor(o[:], o_bank[c][:], res_t[:, :, cols(c)], ALU.add)
            nc.sync.dma_start(out_rows[:, :, cols(c)], o[:])
            leave(c in CAST_V, woven(o_bf[:, c * PACK * CH : (c + 1) * PACK * CH]), by_fours(o[:]))
            for c0, c1 in QO:
                if c == c1 - 1:
                    quantize(o_c[:, c0 * CH : c1 * CH], o_s[:, c0 * CH : c1 * CH], o_bf[:, c0 * PACK * CH : c1 * PACK * CH])
            if c >= NCH - 2:
                done = slice(0, (NCH - 1) * CH) if c == NCH - 2 else cols(c)
                nc.sync.dma_start(words_i32(out_1)[:, done], o_c[:, done].bitcast(I32))

        for c in range(NCH + LAG):
            if c < NCH:
                second_step(c)
            if c >= LAG:
                hand_out(c - LAG)
        for q in range(4):
            eng = nc.scalar if q % 2 else nc.sync
            eng.dma_start(out_2[0, 4 * q : 4 * q + 4, :].bitcast(I32), o_s[32 * q : 32 * q + 4, :].bitcast(I32))
